import numpy as np
import ml_dtypes


def mxq(x, axis, fmt="e4m3"):
    dtype, down = {"e4m3": (ml_dtypes.float8_e4m3fn, 7), "e5m2": (ml_dtypes.float8_e5m2, 14)}[fmt]
    v = np.moveaxis(np.asarray(x, np.float32).astype(ml_dtypes.bfloat16).astype(np.float64), axis, -1)
    blocks = v.reshape(v.shape[:-1] + (-1, 32))
    amax = np.abs(blocks).max(-1, keepdims=True)
    byte = np.maximum(np.where(amax > 0, np.frexp(amax)[1] - 1 + 127, 0) - down, 1)
    scale = np.exp2(byte - 127.0)
    codes = (blocks / scale).astype(np.float32).astype(dtype).astype(np.float64)
    return np.moveaxis((codes * scale).reshape(v.shape), -1, axis)


WIDE = False


def mx_kscale(k):
    if not WIDE:
        return np.ones(k)
    levels = np.array([10, -10, 5, -5, 0])
    if k % 512:
        return np.exp2(np.random.permutation(np.resize(levels, k // 32))).repeat(32)
    a = np.empty((k // 512, 16))
    for p in range(k // 512):
        a[p, :8] = np.random.permutation(np.resize(levels, 8))
        for g in range(8):
            far = levels[np.abs(levels - a[p, g]) >= 10]
            a[p, g + 8] = far[np.random.randint(len(far))]
    return np.exp2(a.ravel()).repeat(32)


def f64(x):
    return np.asarray(x).astype(np.float64)


def striped(idx):
    return np.tile(idx.reshape(-1, 16).T, (8, 1)).astype(np.uint16)


def unstriped(offs):
    return offs[:16].T.reshape(-1).astype(np.int64)


def striped8(idx):
    return np.concatenate([x.reshape(-1, 16).T for x in idx]).astype(np.uint16)


def runs(offs, k):
    lists = np.stack([offs[16 * r : 16 * r + 16].T.reshape(-1) for r in range(8)]).astype(np.int64)
    return lists[np.arange(k) % 512 // 64]


def pack_weight(w):
    k, n = w.shape
    w = f64(np.asarray(w, np.float32).astype(ml_dtypes.bfloat16)).reshape(k // 32, 32, n)
    amax = np.abs(w).max(1)
    byte = np.clip(np.where(amax > 0, np.frexp(amax)[1] - 1 + 127 - 7, 1), 1, 254)
    scaled = (w * np.exp2(127.0 - byte)[:, None, :]).reshape(k, n).astype(np.float32)
    words = np.ascontiguousarray(scaled.reshape(k // 512, 128, 4, n).transpose(0, 1, 3, 2)).astype(ml_dtypes.float8_e4m3fn).view(np.uint8)
    return words, np.ascontiguousarray(byte.astype(np.uint8).reshape(k // 512, 16, n))


def unpack_weight(words, scales):
    g, p, n, _ = words.shape
    vals = np.ascontiguousarray(words).view(ml_dtypes.float8_e4m3fn).astype(np.float64) * np.repeat(np.exp2(scales.astype(np.float64) - 127.0), 8, axis=1)[..., None]
    return vals.transpose(0, 1, 3, 2).reshape(g * 512, n)


def sigmoid(v):
    return 1.0 / (1.0 + np.exp(-np.maximum(v, -700.0)))

def planes(y):
    n, m = y.shape
    v = y.astype(np.float32).astype(ml_dtypes.bfloat16).astype(np.float64).reshape(n // 32, 32, m)
    top = np.abs(v).max(1)
    byte = np.clip(np.where(top > 0, np.frexp(top)[1] - 1 + 127 - 7, 1), 1, 254)
    codes = (v * np.exp2(127.0 - byte)[:, None, :]).reshape(n, m).astype(np.float32).astype(ml_dtypes.float8_e4m3fn).view(np.uint8)
    words = codes.reshape(n // 512, 128, 4, m).transpose(0, 1, 3, 2)
    return np.ascontiguousarray(words), np.ascontiguousarray(byte.astype(np.uint8).reshape(n // 512, 16, m))


K, T, S, G, H = 512, 2048, 512, 2048, 512


def setup_inputs():
    n = np.random.standard_normal
    s = mx_kscale(K)[:, None]
    packed_xT = pack_weight(n((K, T)) * s)
    packed_dT = pack_weight(n((K, G)) / s)
    return {
        "x_words": packed_xT[0],
        "x_scales": packed_xT[1],
        "d_words": packed_dT[0],
        "d_scales": packed_dT[1],
        "gs": (np.random.uniform(0.5, 1.5, (K, 1)) * s).astype(np.float32),
        "offs": striped(np.random.permutation(T)[:S]),
        "k1": striped8(np.random.randint(0, G, (8, H))),
        "n1": striped8(np.stack([np.random.permutation(S) for _ in range(8)])),
        "n2": striped8(np.stack([np.random.permutation(S) for _ in range(8)])),
        "n3": striped8(np.stack([np.random.permutation(S) for _ in range(8)])),
    }


def reference(x_words, x_scales, d_words, d_scales, gs, offs, k1, n1, n2, n3):
    d_k1 = unpack_weight(d_words, d_scales)[np.arange(K)[:, None], runs(k1, K)]
    xq = unpack_weight(x_words, x_scales)[:, unstriped(offs)]
    h = 0.0625 * (d_k1.T @ xq)
    z = f64(gs) * (h - (h[np.arange(H)[:, None], runs(n1, H)]))
    h2 = 0.0625 * ((d_k1.T @ mxq(z, 0, "e4m3")))
    out_0 = h2 + (sigmoid(h2[np.arange(H)[:, None], runs(n2, H)])) * (h2[np.arange(H)[:, None], runs(n3, H)] - h2)
    return (out_0,) + planes(out_0)

@@ -1,0 +1,197 @@
+from contextlib import ExitStack
+
+import concourse.mybir as mybir
+
+F32 = mybir.dt.float32
+BF16 = mybir.dt.bfloat16
+I32 = mybir.dt.int32
+U32 = mybir.dt.uint32
+U16 = mybir.dt.uint16
+U8 = mybir.dt.uint8
+FP8X4 = mybir.dt.float8_e4m3fn_x4
+ALU = mybir.AluOpType
+ACT = mybir.ActivationFunctionType
+
+P = 128
+PACK = 4
+TABLE = 2048
+S = 512
+HALF = S // 2
+LIST_COLS = S // 16
+FLOPS = 2 * 2 * 512 * 512 * 512
+
+
+def tile_picked_ringdiftrack_none_po_kernel(
+    tc, x_words, x_scales, d_words, d_scales, gs, offs, k1, n1, n2, n3, out_0, out_1, out_2
+):
+    nc = tc.nc
+    with ExitStack() as ctx:
+        lists = ctx.enter_context(tc.tile_pool(name="lists", bufs=1))
+        keep = ctx.enter_context(tc.tile_pool(name="keep", bufs=1))
+        psum = ctx.enter_context(tc.psum_pool(name="psum", bufs=1))
+
+        def list_tile(name):
+            return lists.tile([P, LIST_COLS], U16, name=name)
+
+        def half_of(list_t, h):
+            return list_t[:, h * LIST_COLS // 2 : (h + 1) * LIST_COLS // 2]
+
+        def cols(h):
+            return slice(h * HALF, (h + 1) * HALF)
+
+        k1_t, offs_t, n1_t, n2_t, n3_t = (list_tile(n) for n in ("k1_t", "offs_t", "n1_t", "n2_t", "n3_t"))
+        d_word_table = keep.tile([P, TABLE], U32, name="d_word_table")
+        x_word_table = keep.tile([P, TABLE], U32, name="x_word_table")
+        d_scale_table = keep.tile([P, TABLE], U8, name="d_scale_table")
+        x_scale_table = keep.tile([P, TABLE], U8, name="x_scale_table")
+        d_plane = keep.tile([P, S], U8, name="d_plane", align_bytes=64)
+        gs_t = keep.tile([P, PACK], F32, name="gs_t")
+        gain = keep.tile([P, PACK], F32, name="gain")
+
+        nc.vector.memset(d_scale_table[:].bitcast(I32), 0)
+        nc.vector.memset(x_scale_table[:].bitcast(I32), 0)
+        nc.vector.memset(d_plane[:].bitcast(I32), 0)
+
+        nc.sync.dma_start(k1_t[:], k1)
+        nc.scalar.dma_start(d_scale_table[:].bitcast(I32)[0:P:8, :], d_scales[0].bitcast(I32))
+        nc.sync.dma_start(offs_t[:], offs)
+        nc.sync.dma_start(n1_t[:], n1)
+        nc.sync.dma_start(d_word_table[:].bitcast(I32), d_words[0].rearrange("p n t -> p (n t)").bitcast(I32))
+        nc.sync.dma_start(x_word_table[:].bitcast(I32), x_words[0].rearrange("p n t -> p (n t)").bitcast(I32))
+        nc.sync.dma_start(n2_t[:], n2)
+        nc.sync.dma_start(n3_t[:], n3)
+        for q in range(4):
+            nc.gpsimd.dma_start(
+                x_scale_table[:].bitcast(I32)[32 * q : 32 * q + 4, :], x_scales[0, 4 * q : 4 * q + 4, :].bitcast(I32)
+            )
+        nc.gpsimd.dma_start(gs_t[:], gs.rearrange("(p t) o -> p (t o)", t=PACK))
+        nc.scalar.activation(gain[:], gs_t[:], ACT.Copy, scale=-0.0625)
+
+        d_scales_picked = keep.tile([P, S], U8, name="d_scales_picked")
+        d_scales_dealt = keep.tile([P, S], U8, name="d_scales_dealt")
+        nc.vector.tensor_copy(d_scales_picked[:], d_scale_table[:].indirect(k1_t[:]))
+        nc.vector.tensor_copy(
+            d_scales_dealt[:].rearrange("p (t c i) -> p c t i", t=PACK, i=16),
+            d_scales_picked[:].rearrange("p (c i t) -> p c t i", t=PACK, i=16),
+        )
+        for a in range(4):
+            nc.scalar.dma_start(d_plane[:].bitcast(I32)[a:P:32, :], d_scales_dealt[:].bitcast(I32)[8 * a : P : 32, :])
+
+        d_words_picked = keep.tile([P, S], U32, name="d_words_picked")
+        d_codes = keep.tile([P, S], U32, name="d_codes", align_bytes=64)
+        nc.vector.tensor_copy(d_words_picked[:], d_word_table[:].indirect(k1_t[:]))
+        nc.vector.tensor_copy(
+            d_codes[:].bitcast(I32).rearrange("p (t c i) -> p c t i", t=PACK, i=4),
+            d_words_picked[:].bitcast(I32).rearrange("p (c i t) -> p c t i", t=PACK, i=4),
+        )
+
+        def product(h, codes, plane):
+            banks = []
+            for t in range(PACK):
+                bank = psum.tile([P, S], F32, name=f"bank{t}{h}")
+                rows = slice(t * P, (t + 1) * P)
+                nc.tensor.matmul_mx(
+                    out=bank[:, :HALF],
+                    lhsT=d_codes[:, rows].bitcast(FP8X4),
+                    lhsT_scale=d_plane[:, rows],
+                    rhs=codes.bitcast(FP8X4),
+                    rhs_scale=plane,
+                    start=True,
+                    stop=True,
+                )
+                banks.append(bank)
+            return banks
+
+        first = []
+        for h in range(2):
+            x_plane = keep.tile([P, HALF], U8, name=f"x_plane{h}", align_bytes=64)
+            x_codes = keep.tile([P, HALF], U32, name=f"x_codes{h}", align_bytes=64)
+            nc.vector.tensor_copy(x_plane[:], x_scale_table[:].indirect(half_of(offs_t, h)))
+            nc.vector.tensor_copy(x_codes[:], x_word_table[:].indirect(half_of(offs_t, h)))
+            first.append(product(h, x_codes[:], x_plane[:]))
+
+        gh = [keep.tile([P, S], F32, name=f"gh{t}") for t in range(PACK)]
+        gh_own = [[keep.tile([P, HALF], F32, name=f"gh_own{t}{h}") for h in range(2)] for t in range(PACK)]
+        z = [keep.tile([P, PACK, HALF], F32, name=f"z{h}") for h in range(2)]
+
+        def leave_first(out, t, h):
+            nc.scalar.activation(out, first[h][t][:, :HALF], ACT.Copy, scale=gain[:, t : t + 1])
+
+        def difference(t, h):
+            nc.vector.tensor_tensor(z[h][:, t, :], gh[t][:].indirect(half_of(n1_t, h)), gh_own[t][h][:], ALU.subtract)
+
+        def interleave(copy, name, planar):
+            packed = keep.tile([P, PACK * HALF], BF16, name=name, align_bytes=64)
+            copy(
+                packed[:].rearrange("p (c i t) -> p c t i", t=PACK, i=4),
+                planar[:].rearrange("p t (c i) -> p c t i", i=4),
+            )
+            return packed
+
+        for t in range(PACK):
+            leave_first(gh[t][:, cols(0)], t, 0)
+            leave_first(gh_own[t][0][:], t, 0)
+            leave_first(gh[t][:, cols(1)], t, 1)
+            difference(t, 0)
+        for t in range(PACK):
+            leave_first(gh_own[t][1][:], t, 1)
+        z_codes = [keep.tile([P, HALF], U32, name=f"z_codes{h}", align_bytes=64) for h in range(2)]
+        z_plane = [keep.tile([P, HALF], U8, name=f"z_plane{h}", align_bytes=64) for h in range(2)]
+        h2 = [keep.tile([P, S], F32, name=f"h2{t}") for t in range(PACK)]
+
+        z_packed0 = interleave(nc.scalar.copy, "z_packed0", z[0])
+        for t in range(PACK - 1):
+            difference(t, 1)
+        nc.vector.quantize_mx(z_codes[0][:].bitcast(FP8X4), z_plane[0][:], z_packed0[:])
+        difference(PACK - 1, 1)
+        second0 = product(0, z_codes[0][:], z_plane[0][:])
+        for t in range(PACK):
+            nc.scalar.activation(h2[t][:, cols(0)], second0[t][:, :HALF], ACT.Copy, scale=0.0625)
+        z_packed1 = interleave(nc.vector.tensor_copy, "z_packed1", z[1])
+        nc.vector.quantize_mx(z_codes[1][:].bitcast(FP8X4), z_plane[1][:], z_packed1[:])
+        second1 = product(1, z_codes[1][:], z_plane[1][:])
+        nc.scalar.activation(h2[0][:, cols(1)], second1[0][:, :HALF], ACT.Copy, scale=0.0625)
+        for t in range(1, PACK):
+            nc.vector.tensor_scalar(h2[t][:, cols(1)], second1[t][:, :HALF], 0.0625, None, ALU.mult)
+
+        result = [keep.tile([P, PACK, HALF], F32, name=f"result{h}") for h in range(2)]
+        out_codes = keep.tile([P, S], U32, name="out_codes", align_bytes=64)
+        out_plane = keep.tile([P, S], U8, name="out_plane", align_bytes=64)
+        out_rows = out_0.rearrange("(p t) c -> p t c", t=PACK)
+        out_words = out_1[0].rearrange("p n t -> p (n t)").bitcast(I32)
+
+        def blend_parts(t, h):
+            gate = keep.tile([P, HALF], F32, name=f"gate{t}{h}")
+            pulled = keep.tile([P, HALF], F32, name=f"pulled{t}{h}")
+            kept = keep.tile([P, HALF], F32, name=f"kept{t}{h}")
+            nc.scalar.activation(gate[:], h2[t][:].indirect(half_of(n2_t, h)), ACT.Sigmoid)
+            nc.vector.tensor_tensor(pulled[:], h2[t][:].indirect(half_of(n3_t, h)), gate[:], ALU.mult)
+            nc.vector.scalar_tensor_tensor(kept[:], gate[:], 1.0, h2[t][:, cols(h)], ALU.subtract, ALU.mult)
+            return pulled, kept
+
+        def blend_end(t, h, pulled, kept):
+            nc.vector.tensor_tensor(result[h][:, t, :], pulled[:], kept[:], ALU.subtract)
+            nc.sync.dma_start(out_rows[:, t, cols(h)], result[h][:, t, :])
+
+        def planes(h, packed):
+            nc.vector.quantize_mx(out_codes[:, cols(h)].bitcast(FP8X4), out_plane[:, cols(h)], packed[:])
+            nc.sync.dma_start(out_words[:, cols(h)], out_codes[:, cols(h)].bitcast(I32))
+
+        steps = [(t, h) for h in range(2) for t in range(PACK)]
+        waiting = None
+        packed0 = None
+        for t, h in steps:
+            parts = blend_parts(t, h)
+            if waiting is not None:
+                blend_end(*waiting)
+            waiting = (t, h) + parts
+            if (t, h) == (0, 1):
+                packed0 = interleave(nc.scalar.copy, "out_packed0", result[0])
+            if (t, h) == (2, 1):
+                planes(0, packed0)
+        blend_end(*waiting)
+        planes(1, interleave(nc.vector.tensor_copy, "out_packed1", result[1]))
+        for q in range(4):
+            nc.scalar.dma_start(
+                out_2[0, 4 * q : 4 * q + 4, :].bitcast(I32), out_plane[:].bitcast(I32)[32 * q : 32 * q + 4, :]
+            )

@@ -50,32 +50,33 @@ def tile_picked_ringdiftrack_none_po_kernel(
 
         nc.vector.memset(d_scale_table[:].bitcast(I32), 0)
         nc.vector.memset(x_scale_table[:].bitcast(I32), 0)
-        nc.vector.memset(d_plane[:].bitcast(I32), 0)
+        warm = keep.tile([P, 2], F32, name="warm")
+        nc.vector.memset(warm[:, 0:1], 0.0)
 
         nc.sync.dma_start(k1_t[:], k1)
-        nc.scalar.dma_start(d_scale_table[:].bitcast(I32)[0:P:8, :], d_scales[0].bitcast(I32))
+        nc.sync.dma_start(d_scale_table[:].bitcast(I32)[0:P:8, :], d_scales[0].bitcast(I32))
         nc.sync.dma_start(offs_t[:], offs)
-        nc.sync.dma_start(n1_t[:], n1)
         nc.sync.dma_start(d_word_table[:].bitcast(I32), d_words[0].rearrange("p n t -> p (n t)").bitcast(I32))
+        nc.sync.dma_start(n1_t[:], n1)
         nc.sync.dma_start(x_word_table[:].bitcast(I32), x_words[0].rearrange("p n t -> p (n t)").bitcast(I32))
         nc.sync.dma_start(n2_t[:], n2)
         nc.sync.dma_start(n3_t[:], n3)
         for q in range(4):
-            nc.gpsimd.dma_start(
+            nc.scalar.dma_start(
                 x_scale_table[:].bitcast(I32)[32 * q : 32 * q + 4, :], x_scales[0, 4 * q : 4 * q + 4, :].bitcast(I32)
             )
+        nc.scalar.activation(warm[:, 1:2], warm[:, 0:1], ACT.Sigmoid)
         nc.gpsimd.dma_start(gs_t[:], gs.rearrange("(p t) o -> p (t o)", t=PACK))
         nc.scalar.activation(gain[:], gs_t[:], ACT.Copy, scale=-0.0625)
 
         d_scales_picked = keep.tile([P, S], U8, name="d_scales_picked")
-        d_scales_dealt = keep.tile([P, S], U8, name="d_scales_dealt")
         nc.vector.tensor_copy(d_scales_picked[:], d_scale_table[:].indirect(k1_t[:]))
         nc.vector.tensor_copy(
-            d_scales_dealt[:].rearrange("p (t c i) -> p c t i", t=PACK, i=16),
+            d_plane[:].rearrange("p (t c i) -> p c t i", t=PACK, i=16),
             d_scales_picked[:].rearrange("p (c i t) -> p c t i", t=PACK, i=16),
         )
-        for a in range(4):
-            nc.scalar.dma_start(d_plane[:].bitcast(I32)[a:P:32, :], d_scales_dealt[:].bitcast(I32)[8 * a : P : 32, :])
+        for a in range(1, 4):
+            nc.scalar.dma_start(d_plane[:].bitcast(I32)[a:P:32, :], d_plane[:].bitcast(I32)[8 * a : P : 32, :])
 
         d_words_picked = keep.tile([P, S], U32, name="d_words_picked")
         d_codes = keep.tile([P, S], U32, name="d_codes", align_bytes=64)
@@ -131,7 +132,11 @@ def tile_picked_ringdiftrack_none_po_kernel(
         for t in range(PACK):
             leave_first(gh[t][:, cols(0)], t, 0)
             leave_first(gh_own[t][0][:], t, 0)
+        for t in range(2):
+            nc.vector.tensor_scalar(gh[t][:, cols(1)], first[1][t][:, :HALF], gain[:, t : t + 1], None, ALU.mult)
+        for t in range(2, PACK):
             leave_first(gh[t][:, cols(1)], t, 1)
+        for t in range(PACK):
             difference(t, 0)
         for t in range(PACK):
             leave_first(gh_own[t][1][:], t, 1)
@@ -160,13 +165,14 @@ def tile_picked_ringdiftrack_none_po_kernel(
         out_rows = out_0.rearrange("(p t) c -> p t c", t=PACK)
         out_words = out_1[0].rearrange("p n t -> p (n t)").bitcast(I32)
 
-        def blend_parts(t, h):
-            gate = keep.tile([P, HALF], F32, name=f"gate{t}{h}")
+        first_gate = keep.tile([P, HALF], F32, name="first_gate")
+
+        def blend_parts(t, h, gate):
             pulled = keep.tile([P, HALF], F32, name=f"pulled{t}{h}")
             kept = keep.tile([P, HALF], F32, name=f"kept{t}{h}")
-            nc.scalar.activation(gate[:], h2[t][:].indirect(half_of(n2_t, h)), ACT.Sigmoid)
-            nc.vector.tensor_tensor(pulled[:], h2[t][:].indirect(half_of(n3_t, h)), gate[:], ALU.mult)
-            nc.vector.scalar_tensor_tensor(kept[:], gate[:], 1.0, h2[t][:, cols(h)], ALU.subtract, ALU.mult)
+            nc.scalar.activation(gate, h2[t][:].indirect(half_of(n2_t, h)), ACT.Sigmoid)
+            nc.vector.tensor_tensor(pulled[:], h2[t][:].indirect(half_of(n3_t, h)), gate, ALU.mult)
+            nc.vector.scalar_tensor_tensor(kept[:], gate, 1.0, h2[t][:, cols(h)], ALU.subtract, ALU.mult)
             return pulled, kept
 
         def blend_end(t, h, pulled, kept):
@@ -181,7 +187,7 @@ def tile_picked_ringdiftrack_none_po_kernel(
         waiting = None
         packed0 = None
         for t, h in steps:
-            parts = blend_parts(t, h)
+            parts = blend_parts(t, h, first_gate[:] if waiting is None else result[waiting[1]][:, waiting[0], :])
             if waiting is not None:
                 blend_end(*waiting)
             waiting = (t, h) + parts
@@ -192,6 +198,6 @@ def tile_picked_ringdiftrack_none_po_kernel(
         blend_end(*waiting)
         planes(1, interleave(nc.vector.tensor_copy, "out_packed1", result[1]))
         for q in range(4):
-            nc.scalar.dma_start(
+            (nc.scalar if q % 2 else nc.sync).dma_start(
                 out_2[0, 4 * q : 4 * q + 4, :].bitcast(I32), out_plane[:].bitcast(I32)[32 * q : 32 * q + 4, :]
             )

@@ -18,6 +18,7 @@ TABLE = 2048
 S = 512
 HALF = S // 2
 LIST_COLS = S // 16
+VECTOR_SHARE = 168
 FLOPS = 2 * 2 * 512 * 512 * 512
 
 
@@ -58,15 +59,15 @@ def tile_picked_ringdiftrack_none_po_kernel(
         nc.sync.dma_start(offs_t[:], offs)
         nc.sync.dma_start(d_word_table[:].bitcast(I32), d_words[0].rearrange("p n t -> p (n t)").bitcast(I32))
         nc.sync.dma_start(n1_t[:], n1)
-        nc.sync.dma_start(x_word_table[:].bitcast(I32), x_words[0].rearrange("p n t -> p (n t)").bitcast(I32))
         nc.sync.dma_start(n2_t[:], n2)
+        nc.sync.dma_start(x_word_table[:].bitcast(I32), x_words[0].rearrange("p n t -> p (n t)").bitcast(I32))
         nc.sync.dma_start(n3_t[:], n3)
         for q in range(4):
             nc.scalar.dma_start(
                 x_scale_table[:].bitcast(I32)[32 * q : 32 * q + 4, :], x_scales[0, 4 * q : 4 * q + 4, :].bitcast(I32)
             )
         nc.scalar.activation(warm[:, 1:2], warm[:, 0:1], ACT.Sigmoid)
-        nc.gpsimd.dma_start(gs_t[:], gs.rearrange("(p t) o -> p (t o)", t=PACK))
+        nc.sync.dma_start(gs_t[:], gs.rearrange("(p t) o -> p (t o)", t=PACK))
         nc.scalar.activation(gain[:], gs_t[:], ACT.Copy, scale=-0.0625)
 
         d_scales_picked = keep.tile([P, S], U8, name="d_scales_picked")
@@ -78,7 +79,7 @@ def tile_picked_ringdiftrack_none_po_kernel(
         for a in range(1, 4):
             nc.scalar.dma_start(d_plane[:].bitcast(I32)[a:P:32, :], d_plane[:].bitcast(I32)[8 * a : P : 32, :])
 
-        d_words_picked = keep.tile([P, S], U32, name="d_words_picked")
+        d_words_picked = keep.tile([P, S], U32, name="d_words_picked", tag="picked", align_bytes=64)
         d_codes = keep.tile([P, S], U32, name="d_codes", align_bytes=64)
         nc.vector.tensor_copy(d_words_picked[:], d_word_table[:].indirect(k1_t[:]))
         nc.vector.tensor_copy(
@@ -104,12 +105,12 @@ def tile_picked_ringdiftrack_none_po_kernel(
             return banks
 
         first = []
+        x_plane = keep.tile([P, S], U8, name="x_plane", tag="picked", align_bytes=64)
+        nc.vector.tensor_copy(x_plane[:], x_scale_table[:].indirect(offs_t[:]))
         for h in range(2):
-            x_plane = keep.tile([P, HALF], U8, name=f"x_plane{h}", align_bytes=64)
             x_codes = keep.tile([P, HALF], U32, name=f"x_codes{h}", align_bytes=64)
-            nc.vector.tensor_copy(x_plane[:], x_scale_table[:].indirect(half_of(offs_t, h)))
             nc.vector.tensor_copy(x_codes[:], x_word_table[:].indirect(half_of(offs_t, h)))
-            first.append(product(h, x_codes[:], x_plane[:]))
+            first.append(product(h, x_codes[:], x_plane[:, cols(h)]))
 
         gh = [keep.tile([P, S], F32, name=f"gh{t}") for t in range(PACK)]
         gh_own = [[keep.tile([P, HALF], F32, name=f"gh_own{t}{h}") for h in range(2)] for t in range(PACK)]
@@ -121,13 +122,15 @@ def tile_picked_ringdiftrack_none_po_kernel(
         def difference(t, h):
             nc.vector.tensor_tensor(z[h][:, t, :], gh[t][:].indirect(half_of(n1_t, h)), gh_own[t][h][:], ALU.subtract)
 
-        def interleave(copy, name, planar):
-            packed = keep.tile([P, PACK * HALF], BF16, name=name, align_bytes=64)
-            copy(
-                packed[:].rearrange("p (c i t) -> p c t i", t=PACK, i=4),
-                planar[:].rearrange("p t (c i) -> p c t i", i=4),
-            )
-            return packed
+        def interleave(name, planar, on_vector):
+            packed = keep.tile([P, HALF, PACK], BF16, name=name, align_bytes=64)
+            for copy, part in ((nc.vector.tensor_copy, slice(0, on_vector)), (nc.scalar.copy, slice(on_vector, HALF))):
+                if part.start < part.stop:
+                    copy(
+                        packed[:, part, :].rearrange("p (c i) t -> p c t i", i=4),
+                        planar[:, :, part].rearrange("p t (c i) -> p c t i", i=4),
+                    )
+            return packed[:].rearrange("p c t -> p (c t)")
 
         for t in range(PACK):
             leave_first(gh[t][:, cols(0)], t, 0)
@@ -144,16 +147,17 @@ def tile_picked_ringdiftrack_none_po_kernel(
         z_plane = [keep.tile([P, HALF], U8, name=f"z_plane{h}", align_bytes=64) for h in range(2)]
         h2 = [keep.tile([P, S], F32, name=f"h2{t}") for t in range(PACK)]
 
-        z_packed0 = interleave(nc.scalar.copy, "z_packed0", z[0])
-        for t in range(PACK - 1):
+        z_packed0 = interleave("z_packed0", z[0], 0)
+        for t in range(2):
             difference(t, 1)
-        nc.vector.quantize_mx(z_codes[0][:].bitcast(FP8X4), z_plane[0][:], z_packed0[:])
-        difference(PACK - 1, 1)
+        nc.vector.quantize_mx(z_codes[0][:].bitcast(FP8X4), z_plane[0][:], z_packed0)
+        for t in range(2, PACK):
+            difference(t, 1)
         second0 = product(0, z_codes[0][:], z_plane[0][:])
+        z_packed1 = interleave("z_packed1", z[1], VECTOR_SHARE)
         for t in range(PACK):
             nc.scalar.activation(h2[t][:, cols(0)], second0[t][:, :HALF], ACT.Copy, scale=0.0625)
-        z_packed1 = interleave(nc.vector.tensor_copy, "z_packed1", z[1])
-        nc.vector.quantize_mx(z_codes[1][:].bitcast(FP8X4), z_plane[1][:], z_packed1[:])
+        nc.vector.quantize_mx(z_codes[1][:].bitcast(FP8X4), z_plane[1][:], z_packed1)
         second1 = product(1, z_codes[1][:], z_plane[1][:])
         nc.scalar.activation(h2[0][:, cols(1)], second1[0][:, :HALF], ACT.Copy, scale=0.0625)
         for t in range(1, PACK):
@@ -180,7 +184,7 @@ def tile_picked_ringdiftrack_none_po_kernel(
             nc.sync.dma_start(out_rows[:, t, cols(h)], result[h][:, t, :])
 
         def planes(h, packed):
-            nc.vector.quantize_mx(out_codes[:, cols(h)].bitcast(FP8X4), out_plane[:, cols(h)], packed[:])
+            nc.vector.quantize_mx(out_codes[:, cols(h)].bitcast(FP8X4), out_plane[:, cols(h)], packed)
             nc.sync.dma_start(out_words[:, cols(h)], out_codes[:, cols(h)].bitcast(I32))
 
         steps = [(t, h) for h in range(2) for t in range(PACK)]
@@ -192,11 +196,11 @@ def tile_picked_ringdiftrack_none_po_kernel(
                 blend_end(*waiting)
             waiting = (t, h) + parts
             if (t, h) == (0, 1):
-                packed0 = interleave(nc.scalar.copy, "out_packed0", result[0])
+                packed0 = interleave("out_packed0", result[0], 0)
             if (t, h) == (2, 1):
                 planes(0, packed0)
         blend_end(*waiting)
-        planes(1, interleave(nc.vector.tensor_copy, "out_packed1", result[1]))
+        planes(1, interleave("out_packed1", result[1], VECTOR_SHARE))
         for q in range(4):
             (nc.scalar if q % 2 else nc.sync).dma_start(
                 out_2[0, 4 * q : 4 * q + 4, :].bitcast(I32), out_plane[:].bitcast(I32)[32 * q : 32 * q + 4, :]

@@ -87,56 +87,59 @@ def tile_picked_ringdiftrack_none_po_kernel(
             d_words_picked[:].bitcast(I32).rearrange("p (c i t) -> p c t i", t=PACK, i=4),
         )
 
-        def product(h, codes, plane):
-            banks = []
-            for t in range(PACK):
-                bank = psum.tile([P, S], F32, name=f"bank{t}{h}")
-                rows = slice(t * P, (t + 1) * P)
-                nc.tensor.matmul_mx(
-                    out=bank[:, :HALF],
-                    lhsT=d_codes[:, rows].bitcast(FP8X4),
-                    lhsT_scale=d_plane[:, rows],
-                    rhs=codes.bitcast(FP8X4),
-                    rhs_scale=plane,
-                    start=True,
-                    stop=True,
-                )
-                banks.append(bank)
-            return banks
+        def product(t, h, codes, plane):
+            bank = psum.tile([P, S], F32, name=f"bank{t}{h}")
+            rows = slice(t * P, (t + 1) * P)
+            nc.tensor.matmul_mx(
+                out=bank[:, :HALF],
+                lhsT=d_codes[:, rows].bitcast(FP8X4),
+                lhsT_scale=d_plane[:, rows],
+                rhs=codes.bitcast(FP8X4),
+                rhs_scale=plane,
+                start=True,
+                stop=True,
+            )
+            return bank[:, :HALF]
 
-        first = []
+        x_codes = [keep.tile([P, HALF], U32, name=f"x_codes{h}", align_bytes=64) for h in range(2)]
         x_plane = keep.tile([P, S], U8, name="x_plane", tag="picked", align_bytes=64)
         nc.vector.tensor_copy(x_plane[:], x_scale_table[:].indirect(offs_t[:]))
         for h in range(2):
-            x_codes = keep.tile([P, HALF], U32, name=f"x_codes{h}", align_bytes=64)
-            nc.vector.tensor_copy(x_codes[:], x_word_table[:].indirect(half_of(offs_t, h)))
-            first.append(product(h, x_codes[:], x_plane[:, cols(h)]))
+            nc.vector.tensor_copy(x_codes[h][:], x_word_table[:].indirect(half_of(offs_t, h)))
+        first = {}
+        for pair in range(2):
+            for h in range(2):
+                for t in (2 * pair, 2 * pair + 1):
+                    first[t, h] = product(t, h, x_codes[h][:], x_plane[:, cols(h)])
 
         gh = [keep.tile([P, S], F32, name=f"gh{t}") for t in range(PACK)]
         gh_own = [[keep.tile([P, HALF], F32, name=f"gh_own{t}{h}") for h in range(2)] for t in range(PACK)]
-        z = [keep.tile([P, PACK, HALF], F32, name=f"z{h}") for h in range(2)]
+        z = [keep.tile([P, PACK * HALF], F32, name=f"z{h}", align_bytes=64) for h in range(2)]
 
         def leave_first(out, t, h):
-            nc.scalar.activation(out, first[h][t][:, :HALF], ACT.Copy, scale=gain[:, t : t + 1])
+            nc.scalar.activation(out, first[t, h], ACT.Copy, scale=gain[:, t : t + 1])
 
         def difference(t, h):
-            nc.vector.tensor_tensor(z[h][:, t, :], gh[t][:].indirect(half_of(n1_t, h)), gh_own[t][h][:], ALU.subtract)
+            nc.vector.tensor_tensor(z[h][:, t * HALF : (t + 1) * HALF], gh[t][:].indirect(half_of(n1_t, h)), gh_own[t][h][:], ALU.subtract)
 
-        def interleave(name, planar, on_vector):
-            packed = keep.tile([P, HALF, PACK], BF16, name=name, align_bytes=64)
+        def packed_tile(name):
+            return keep.tile([P, HALF * PACK], BF16, name=name, align_bytes=64)[:]
+
+        def interleave(flat, planar, on_vector):
+            packed = flat.rearrange("p (c t) -> p c t", t=PACK)
             for copy, part in ((nc.vector.tensor_copy, slice(0, on_vector)), (nc.scalar.copy, slice(on_vector, HALF))):
                 if part.start < part.stop:
                     copy(
                         packed[:, part, :].rearrange("p (c i) t -> p c t i", i=4),
                         planar[:, :, part].rearrange("p t (c i) -> p c t i", i=4),
                     )
-            return packed[:].rearrange("p c t -> p (c t)")
+            return flat
 
         for t in range(PACK):
             leave_first(gh[t][:, cols(0)], t, 0)
             leave_first(gh_own[t][0][:], t, 0)
         for t in range(2):
-            nc.vector.tensor_scalar(gh[t][:, cols(1)], first[1][t][:, :HALF], gain[:, t : t + 1], None, ALU.mult)
+            nc.vector.tensor_scalar(gh[t][:, cols(1)], first[t, 1], gain[:, t : t + 1], None, ALU.mult)
         for t in range(2, PACK):
             leave_first(gh[t][:, cols(1)], t, 1)
         for t in range(PACK):
@@ -147,21 +150,20 @@ def tile_picked_ringdiftrack_none_po_kernel(
         z_plane = [keep.tile([P, HALF], U8, name=f"z_plane{h}", align_bytes=64) for h in range(2)]
         h2 = [keep.tile([P, S], F32, name=f"h2{t}") for t in range(PACK)]
 
-        z_packed0 = interleave("z_packed0", z[0], 0)
+        z_packed0 = interleave(z[1][:, 2 * HALF :].bitcast(BF16), z[0][:].rearrange("p (t c) -> p t c", t=PACK), 0)
         for t in range(2):
             difference(t, 1)
         nc.vector.quantize_mx(z_codes[0][:].bitcast(FP8X4), z_plane[0][:], z_packed0)
         for t in range(2, PACK):
             difference(t, 1)
-        second0 = product(0, z_codes[0][:], z_plane[0][:])
-        z_packed1 = interleave("z_packed1", z[1], VECTOR_SHARE)
+        second0 = [product(t, 0, z_codes[0][:], z_plane[0][:]) for t in range(PACK)]
+        z_packed1 = interleave(packed_tile("z_packed1"), z[1][:].rearrange("p (t c) -> p t c", t=PACK), VECTOR_SHARE)
         for t in range(PACK):
-            nc.scalar.activation(h2[t][:, cols(0)], second0[t][:, :HALF], ACT.Copy, scale=0.0625)
+            nc.scalar.activation(h2[t][:, cols(0)], second0[t], ACT.Copy, scale=0.0625)
         nc.vector.quantize_mx(z_codes[1][:].bitcast(FP8X4), z_plane[1][:], z_packed1)
-        second1 = product(1, z_codes[1][:], z_plane[1][:])
-        nc.scalar.activation(h2[0][:, cols(1)], second1[0][:, :HALF], ACT.Copy, scale=0.0625)
-        for t in range(1, PACK):
-            nc.vector.tensor_scalar(h2[t][:, cols(1)], second1[t][:, :HALF], 0.0625, None, ALU.mult)
+        second1 = [product(t, 1, z_codes[1][:], z_plane[1][:]) for t in range(PACK)]
+        nc.scalar.activation(h2[0][:, cols(1)], second1[0], ACT.Copy, scale=0.0625)
+        nc.vector.tensor_scalar(h2[1][:, cols(1)], second1[1], 0.0625, None, ALU.mult)
 
         result = [keep.tile([P, PACK, HALF], F32, name=f"result{h}") for h in range(2)]
         out_codes = keep.tile([P, S], U32, name="out_codes", align_bytes=64)
@@ -175,7 +177,12 @@ def tile_picked_ringdiftrack_none_po_kernel(
             pulled = keep.tile([P, HALF], F32, name=f"pulled{t}{h}")
             kept = keep.tile([P, HALF], F32, name=f"kept{t}{h}")
             nc.scalar.activation(gate, h2[t][:].indirect(half_of(n2_t, h)), ACT.Sigmoid)
-            nc.vector.tensor_tensor(pulled[:], h2[t][:].indirect(half_of(n3_t, h)), gate, ALU.mult)
+            if (t, h) == (0, 0):
+                fetched = keep.tile([P, HALF], F32, name="fetched")
+                nc.vector.tensor_copy(fetched[:], h2[t][:].indirect(half_of(n3_t, h)))
+                nc.vector.tensor_tensor(pulled[:], fetched[:], gate, ALU.mult)
+            else:
+                nc.vector.tensor_tensor(pulled[:], h2[t][:].indirect(half_of(n3_t, h)), gate, ALU.mult)
             nc.vector.scalar_tensor_tensor(kept[:], gate, 1.0, h2[t][:, cols(h)], ALU.subtract, ALU.mult)
             return pulled, kept
 
@@ -191,16 +198,18 @@ def tile_picked_ringdiftrack_none_po_kernel(
         waiting = None
         packed0 = None
         for t, h in steps:
+            if h == 0 and t >= 2:
+                nc.scalar.activation(h2[t][:, cols(1)], second1[t], ACT.Copy, scale=0.0625)
             parts = blend_parts(t, h, first_gate[:] if waiting is None else result[waiting[1]][:, waiting[0], :])
             if waiting is not None:
                 blend_end(*waiting)
             waiting = (t, h) + parts
             if (t, h) == (0, 1):
-                packed0 = interleave("out_packed0", result[0], 0)
+                packed0 = interleave(packed_tile("out_packed0"), result[0][:], 0)
             if (t, h) == (2, 1):
                 planes(0, packed0)
         blend_end(*waiting)
-        planes(1, interleave("out_packed1", result[1], VECTOR_SHARE))
+        planes(1, interleave(packed_tile("out_packed1"), result[1][:], VECTOR_SHARE))
         for q in range(4):
             (nc.scalar if q % 2 else nc.sync).dma_start(
                 out_2[0, 4 * q : 4 * q + 4, :].bitcast(I32), out_plane[:].bitcast(I32)[32 * q : 32 * q + 4, :]

@@ -14,11 +14,18 @@ ACT = mybir.ActivationFunctionType
 
 P = 128
 PACK = 4
+LAST = PACK - 1
+QUADRANT = 32
+BLOCK_PARTITIONS = 8
 TABLE = 2048
 S = 512
 HALF = S // 2
 LIST_COLS = S // 16
+LINE = 16
+RUN = 4
+SIXTEENTH = 0.0625
 VECTOR_SHARE = 168
+VECTOR_BANKS = 2
 FLOPS = 2 * 2 * 512 * 512 * 512
 
 
@@ -34,11 +41,14 @@ def tile_picked_ringdiftrack_none_po_kernel(
         def list_tile(name):
             return lists.tile([P, LIST_COLS], U16, name=name)
 
-        def half_of(list_t, h):
-            return list_t[:, h * LIST_COLS // 2 : (h + 1) * LIST_COLS // 2]
+        def half_of(list_t, half):
+            return list_t[:, half * LIST_COLS // 2 : (half + 1) * LIST_COLS // 2]
 
-        def cols(h):
-            return slice(h * HALF, (h + 1) * HALF)
+        def cols(half):
+            return slice(half * HALF, (half + 1) * HALF)
+
+        def word_rows(words):
+            return words[0].rearrange("p n t -> p (n t)").bitcast(I32)
 
         k1_t, offs_t, n1_t, n2_t, n3_t = (list_tile(n) for n in ("k1_t", "offs_t", "n1_t", "n2_t", "n3_t"))
         d_word_table = keep.tile([P, TABLE], U32, name="d_word_table")
@@ -55,45 +65,49 @@ def tile_picked_ringdiftrack_none_po_kernel(
         nc.vector.memset(warm[:, 0:1], 0.0)
 
         nc.sync.dma_start(k1_t[:], k1)
-        nc.sync.dma_start(d_scale_table[:].bitcast(I32)[0:P:8, :], d_scales[0].bitcast(I32))
+        nc.sync.dma_start(d_scale_table[:].bitcast(I32)[0:P:BLOCK_PARTITIONS, :], d_scales[0].bitcast(I32))
         nc.sync.dma_start(offs_t[:], offs)
-        nc.sync.dma_start(d_word_table[:].bitcast(I32), d_words[0].rearrange("p n t -> p (n t)").bitcast(I32))
+        nc.sync.dma_start(d_word_table[:].bitcast(I32), word_rows(d_words))
         nc.sync.dma_start(n1_t[:], n1)
+        nc.sync.dma_start(gs_t[:], gs.rearrange("(p t) o -> p (t o)", t=PACK))
+        nc.sync.dma_start(x_word_table[:].bitcast(I32), word_rows(x_words))
         nc.sync.dma_start(n2_t[:], n2)
-        nc.sync.dma_start(x_word_table[:].bitcast(I32), x_words[0].rearrange("p n t -> p (n t)").bitcast(I32))
         nc.sync.dma_start(n3_t[:], n3)
-        for q in range(4):
+        for q in range(P // QUADRANT):
             nc.scalar.dma_start(
-                x_scale_table[:].bitcast(I32)[32 * q : 32 * q + 4, :], x_scales[0, 4 * q : 4 * q + 4, :].bitcast(I32)
+                x_scale_table[:].bitcast(I32)[QUADRANT * q : QUADRANT * q + PACK, :],
+                x_scales[0, PACK * q : PACK * q + PACK, :].bitcast(I32),
             )
         nc.scalar.activation(warm[:, 1:2], warm[:, 0:1], ACT.Sigmoid)
-        nc.sync.dma_start(gs_t[:], gs.rearrange("(p t) o -> p (t o)", t=PACK))
-        nc.scalar.activation(gain[:], gs_t[:], ACT.Copy, scale=-0.0625)
+        nc.scalar.activation(gain[:], gs_t[:], ACT.Copy, scale=-SIXTEENTH)
+
+        def deal(dealt, picked, per_line):
+            nc.vector.tensor_copy(
+                dealt.rearrange("p (t c i) -> p c t i", t=PACK, i=per_line),
+                picked.rearrange("p (c i t) -> p c t i", t=PACK, i=per_line),
+            )
 
         d_scales_picked = keep.tile([P, S], U8, name="d_scales_picked")
         nc.vector.tensor_copy(d_scales_picked[:], d_scale_table[:].indirect(k1_t[:]))
-        nc.vector.tensor_copy(
-            d_plane[:].rearrange("p (t c i) -> p c t i", t=PACK, i=16),
-            d_scales_picked[:].rearrange("p (c i t) -> p c t i", t=PACK, i=16),
-        )
-        for a in range(1, 4):
-            nc.scalar.dma_start(d_plane[:].bitcast(I32)[a:P:32, :], d_plane[:].bitcast(I32)[8 * a : P : 32, :])
+        deal(d_plane[:], d_scales_picked[:], LINE)
+        for a in range(1, PACK):
+            nc.scalar.dma_start(
+                d_plane[:].bitcast(I32)[a:P:QUADRANT, :],
+                d_plane[:].bitcast(I32)[BLOCK_PARTITIONS * a : P : QUADRANT, :],
+            )
 
         d_words_picked = keep.tile([P, S], U32, name="d_words_picked", tag="picked", align_bytes=64)
         d_codes = keep.tile([P, S], U32, name="d_codes", align_bytes=64)
         nc.vector.tensor_copy(d_words_picked[:], d_word_table[:].indirect(k1_t[:]))
-        nc.vector.tensor_copy(
-            d_codes[:].bitcast(I32).rearrange("p (t c i) -> p c t i", t=PACK, i=4),
-            d_words_picked[:].bitcast(I32).rearrange("p (c i t) -> p c t i", t=PACK, i=4),
-        )
+        deal(d_codes[:].bitcast(I32), d_words_picked[:].bitcast(I32), LINE // PACK)
 
-        def product(t, h, codes, plane):
-            bank = psum.tile([P, S], F32, name=f"bank{t}{h}")
-            rows = slice(t * P, (t + 1) * P)
+        def product(t, half, codes, plane):
+            bank = psum.tile([P, S], F32, name=f"bank{t}{half}")
+            dealt = slice(t * P, (t + 1) * P)
             nc.tensor.matmul_mx(
                 out=bank[:, :HALF],
-                lhsT=d_codes[:, rows].bitcast(FP8X4),
-                lhsT_scale=d_plane[:, rows],
+                lhsT=d_codes[:, dealt].bitcast(FP8X4),
+                lhsT_scale=d_plane[:, dealt],
                 rhs=codes.bitcast(FP8X4),
                 rhs_scale=plane,
                 start=True,
@@ -101,116 +115,146 @@ def tile_picked_ringdiftrack_none_po_kernel(
             )
             return bank[:, :HALF]
 
-        x_codes = [keep.tile([P, HALF], U32, name=f"x_codes{h}", align_bytes=64) for h in range(2)]
+        x_codes = [keep.tile([P, HALF], U32, name=f"x_codes{half}", align_bytes=64) for half in range(2)]
         x_plane = keep.tile([P, S], U8, name="x_plane", tag="picked", align_bytes=64)
         nc.vector.tensor_copy(x_plane[:], x_scale_table[:].indirect(offs_t[:]))
-        for h in range(2):
-            nc.vector.tensor_copy(x_codes[h][:], x_word_table[:].indirect(half_of(offs_t, h)))
+        for half in range(2):
+            nc.vector.tensor_copy(x_codes[half][:], x_word_table[:].indirect(half_of(offs_t, half)))
         first = {}
-        for pair in range(2):
-            for h in range(2):
+        for pair in range(PACK // 2):
+            for half in range(2):
                 for t in (2 * pair, 2 * pair + 1):
-                    first[t, h] = product(t, h, x_codes[h][:], x_plane[:, cols(h)])
+                    first[t, half] = product(t, half, x_codes[half][:], x_plane[:, cols(half)])
 
-        gh = [keep.tile([P, S], F32, name=f"gh{t}") for t in range(PACK)]
-        gh_own = [[keep.tile([P, HALF], F32, name=f"gh_own{t}{h}") for h in range(2)] for t in range(PACK)]
-        z = [keep.tile([P, PACK * HALF], F32, name=f"z{h}", align_bytes=64) for h in range(2)]
+        window = [keep.tile([P, S], F32, name=f"window{t}") for t in range(PACK)]
+        z = [keep.tile([P, (PACK + half) * HALF], F32, name=f"z{half}", align_bytes=64) for half in range(2)]
+        own = [
+            [
+                z[0][:, :HALF] if (t, half) == (LAST, 1) else keep.tile([P, HALF], F32, name=f"own{t}{half}")[:]
+                for half in range(2)
+            ]
+            for t in range(PACK)
+        ]
 
-        def leave_first(out, t, h):
-            nc.scalar.activation(out, first[t, h], ACT.Copy, scale=gain[:, t : t + 1])
+        def leave_first(out, t, half):
+            nc.scalar.activation(out, first[t, half], ACT.Copy, scale=gain[:, t : t + 1])
 
-        def difference(t, h):
-            nc.vector.tensor_tensor(z[h][:, t * HALF : (t + 1) * HALF], gh[t][:].indirect(half_of(n1_t, h)), gh_own[t][h][:], ALU.subtract)
+        def difference(t, half):
+            nc.vector.tensor_tensor(
+                z[half][:, t * HALF : (t + 1) * HALF],
+                window[t][:].indirect(half_of(n1_t, half)),
+                own[t][half],
+                ALU.subtract,
+            )
 
-        def packed_tile(name):
+        def z_tiles(half):
+            return z[half][:, : PACK * HALF].rearrange("p (t c) -> p t c", t=PACK)
+
+        def rounded_tile(name):
             return keep.tile([P, HALF * PACK], BF16, name=name, align_bytes=64)[:]
 
-        def interleave(flat, planar, on_vector):
-            packed = flat.rearrange("p (c t) -> p c t", t=PACK)
-            for copy, part in ((nc.vector.tensor_copy, slice(0, on_vector)), (nc.scalar.copy, slice(on_vector, HALF))):
-                if part.start < part.stop:
-                    copy(
-                        packed[:, part, :].rearrange("p (c i) t -> p c t i", i=4),
-                        planar[:, :, part].rearrange("p t (c i) -> p c t i", i=4),
-                    )
-            return flat
+        def interleave(copy, rounded, tiles, part):
+            copy(
+                rounded.rearrange("p (c t) -> p c t", t=PACK)[:, part, :].rearrange("p (c i) t -> p c t i", i=RUN),
+                tiles[:, :, part].rearrange("p t (c i) -> p c t i", i=RUN),
+            )
+
+        def interleave_on_scalar(rounded, tiles):
+            interleave(nc.scalar.copy, rounded, tiles, slice(0, HALF))
+            return rounded
+
+        def interleave_on_both(rounded, tiles):
+            interleave(nc.vector.tensor_copy, rounded, tiles, slice(0, VECTOR_SHARE))
+            interleave(nc.scalar.copy, rounded, tiles, slice(VECTOR_SHARE, HALF))
+            return rounded
 
         for t in range(PACK):
-            leave_first(gh[t][:, cols(0)], t, 0)
-            leave_first(gh_own[t][0][:], t, 0)
-        for t in range(2):
-            nc.vector.tensor_scalar(gh[t][:, cols(1)], first[t, 1], gain[:, t : t + 1], None, ALU.mult)
-        for t in range(2, PACK):
-            leave_first(gh[t][:, cols(1)], t, 1)
+            leave_first(window[t][:, cols(0)], t, 0)
+            leave_first(own[t][0], t, 0)
+            if t < VECTOR_BANKS:
+                nc.vector.tensor_scalar(window[t][:, cols(1)], first[t, 1], gain[:, t : t + 1], None, ALU.mult)
+            else:
+                leave_first(window[t][:, cols(1)], t, 1)
         for t in range(PACK):
             difference(t, 0)
-        for t in range(PACK):
-            leave_first(gh_own[t][1][:], t, 1)
-        z_codes = [keep.tile([P, HALF], U32, name=f"z_codes{h}", align_bytes=64) for h in range(2)]
-        z_plane = [keep.tile([P, HALF], U8, name=f"z_plane{h}", align_bytes=64) for h in range(2)]
+        for t in range(LAST):
+            leave_first(own[t][1], t, 1)
+        z_codes = [keep.tile([P, HALF], U32, name=f"z_codes{half}", align_bytes=64) for half in range(2)]
+        z_plane = [keep.tile([P, HALF], U8, name=f"z_plane{half}", align_bytes=64) for half in range(2)]
         h2 = [keep.tile([P, S], F32, name=f"h2{t}") for t in range(PACK)]
 
-        z_packed0 = interleave(z[1][:, 2 * HALF :].bitcast(BF16), z[0][:].rearrange("p (t c) -> p t c", t=PACK), 0)
-        for t in range(2):
-            difference(t, 1)
-        nc.vector.quantize_mx(z_codes[0][:].bitcast(FP8X4), z_plane[0][:], z_packed0)
-        for t in range(2, PACK):
-            difference(t, 1)
-        second0 = [product(t, 0, z_codes[0][:], z_plane[0][:]) for t in range(PACK)]
-        z_packed1 = interleave(packed_tile("z_packed1"), z[1][:].rearrange("p (t c) -> p t c", t=PACK), VECTOR_SHARE)
-        for t in range(PACK):
-            nc.scalar.activation(h2[t][:, cols(0)], second0[t], ACT.Copy, scale=0.0625)
-        nc.vector.quantize_mx(z_codes[1][:].bitcast(FP8X4), z_plane[1][:], z_packed1)
-        second1 = [product(t, 1, z_codes[1][:], z_plane[1][:]) for t in range(PACK)]
-        nc.scalar.activation(h2[0][:, cols(1)], second1[0], ACT.Copy, scale=0.0625)
-        nc.vector.tensor_scalar(h2[1][:, cols(1)], second1[1], 0.0625, None, ALU.mult)
+        def quantise_z(half, rounded):
+            nc.vector.quantize_mx(z_codes[half][:].bitcast(FP8X4), z_plane[half][:], rounded)
 
-        result = [keep.tile([P, PACK, HALF], F32, name=f"result{h}") for h in range(2)]
+        def second_product(half):
+            return [product(t, half, z_codes[half][:], z_plane[half][:]) for t in range(PACK)]
+
+        def leave_second(t, half, bank):
+            nc.scalar.activation(h2[t][:, cols(half)], bank, ACT.Copy, scale=SIXTEENTH)
+
+        z_rounded0 = interleave_on_scalar(z[1][:, LAST * HALF :].bitcast(BF16), z_tiles(0))
+        leave_first(own[LAST][1], LAST, 1)
+        for t in range(LAST):
+            difference(t, 1)
+        quantise_z(0, z_rounded0)
+        difference(LAST, 1)
+
+        second0 = second_product(0)
+        z_rounded1 = interleave_on_both(rounded_tile("z_rounded1"), z_tiles(1))
+        for t in range(PACK):
+            leave_second(t, 0, second0[t])
+        quantise_z(1, z_rounded1)
+        second1 = second_product(1)
+        leave_second(0, 1, second1[0])
+        nc.vector.tensor_scalar(h2[1][:, cols(1)], second1[1], SIXTEENTH, None, ALU.mult)
+
+        result = [keep.tile([P, PACK, HALF], F32, name=f"result{half}") for half in range(2)]
         out_codes = keep.tile([P, S], U32, name="out_codes", align_bytes=64)
         out_plane = keep.tile([P, S], U8, name="out_plane", align_bytes=64)
         out_rows = out_0.rearrange("(p t) c -> p t c", t=PACK)
-        out_words = out_1[0].rearrange("p n t -> p (n t)").bitcast(I32)
-
+        out_words = word_rows(out_1)
         first_gate = keep.tile([P, HALF], F32, name="first_gate")
 
-        def blend_parts(t, h, gate):
-            pulled = keep.tile([P, HALF], F32, name=f"pulled{t}{h}")
-            kept = keep.tile([P, HALF], F32, name=f"kept{t}{h}")
-            nc.scalar.activation(gate, h2[t][:].indirect(half_of(n2_t, h)), ACT.Sigmoid)
-            if (t, h) == (0, 0):
+        def blend_terms(t, half, gate):
+            pulled = keep.tile([P, HALF], F32, name=f"pulled{t}{half}")
+            kept = keep.tile([P, HALF], F32, name=f"kept{t}{half}")
+            nc.scalar.activation(gate, h2[t][:].indirect(half_of(n2_t, half)), ACT.Sigmoid)
+            if (t, half) == (0, 0):
                 fetched = keep.tile([P, HALF], F32, name="fetched")
-                nc.vector.tensor_copy(fetched[:], h2[t][:].indirect(half_of(n3_t, h)))
+                nc.vector.tensor_copy(fetched[:], h2[t][:].indirect(half_of(n3_t, half)))
                 nc.vector.tensor_tensor(pulled[:], fetched[:], gate, ALU.mult)
             else:
-                nc.vector.tensor_tensor(pulled[:], h2[t][:].indirect(half_of(n3_t, h)), gate, ALU.mult)
-            nc.vector.scalar_tensor_tensor(kept[:], gate, 1.0, h2[t][:, cols(h)], ALU.subtract, ALU.mult)
+                nc.vector.tensor_tensor(pulled[:], h2[t][:].indirect(half_of(n3_t, half)), gate, ALU.mult)
+            nc.vector.scalar_tensor_tensor(kept[:], gate, 1.0, h2[t][:, cols(half)], ALU.subtract, ALU.mult)
             return pulled, kept
 
-        def blend_end(t, h, pulled, kept):
-            nc.vector.tensor_tensor(result[h][:, t, :], pulled[:], kept[:], ALU.subtract)
-            nc.sync.dma_start(out_rows[:, t, cols(h)], result[h][:, t, :])
+        def blend_end(t, half, pulled, kept):
+            nc.vector.tensor_tensor(result[half][:, t, :], pulled[:], kept[:], ALU.subtract)
+            nc.sync.dma_start(out_rows[:, t, cols(half)], result[half][:, t, :])
 
-        def planes(h, packed):
-            nc.vector.quantize_mx(out_codes[:, cols(h)].bitcast(FP8X4), out_plane[:, cols(h)], packed)
-            nc.sync.dma_start(out_words[:, cols(h)], out_codes[:, cols(h)].bitcast(I32))
+        def quantise_out(half, rounded):
+            nc.vector.quantize_mx(out_codes[:, cols(half)].bitcast(FP8X4), out_plane[:, cols(half)], rounded)
+            nc.sync.dma_start(out_words[:, cols(half)], out_codes[:, cols(half)].bitcast(I32))
 
-        steps = [(t, h) for h in range(2) for t in range(PACK)]
-        waiting = None
-        packed0 = None
-        for t, h in steps:
-            if h == 0 and t >= 2:
-                nc.scalar.activation(h2[t][:, cols(1)], second1[t], ACT.Copy, scale=0.0625)
-            parts = blend_parts(t, h, first_gate[:] if waiting is None else result[waiting[1]][:, waiting[0], :])
-            if waiting is not None:
-                blend_end(*waiting)
-            waiting = (t, h) + parts
-            if (t, h) == (0, 1):
-                packed0 = interleave(packed_tile("out_packed0"), result[0][:], 0)
-            if (t, h) == (2, 1):
-                planes(0, packed0)
-        blend_end(*waiting)
-        planes(1, interleave(packed_tile("out_packed1"), result[1][:], VECTOR_SHARE))
-        for q in range(4):
+        gate = first_gate[:]
+        unfinished = []
+        for half in range(2):
+            for t in range(PACK):
+                if half == 0 and t >= 2:
+                    leave_second(t, 1, second1[t])
+                terms = blend_terms(t, half, gate)
+                if unfinished:
+                    blend_end(*unfinished.pop())
+                unfinished.append((t, half) + terms)
+                gate = result[half][:, t, :]
+                if (t, half) == (0, 1):
+                    out_rounded0 = interleave_on_scalar(rounded_tile("out_rounded0"), result[0][:])
+                if (t, half) == (2, 1):
+                    quantise_out(0, out_rounded0)
+        blend_end(*unfinished.pop())
+        quantise_out(1, interleave_on_both(rounded_tile("out_rounded1"), result[1][:]))
+        for q in range(P // QUADRANT):
             (nc.scalar if q % 2 else nc.sync).dma_start(
-                out_2[0, 4 * q : 4 * q + 4, :].bitcast(I32), out_plane[:].bitcast(I32)[32 * q : 32 * q + 4, :]
+                out_2[0, PACK * q : PACK * q + PACK, :].bitcast(I32),
+                out_plane[:].bitcast(I32)[QUADRANT * q : QUADRANT * q + PACK, :],
             )

from contextlib import ExitStack

import concourse.mybir as mybir

F32 = mybir.dt.float32
BF16 = mybir.dt.bfloat16
I32 = mybir.dt.int32
U32 = mybir.dt.uint32
U16 = mybir.dt.uint16
U8 = mybir.dt.uint8
FP8X4 = mybir.dt.float8_e4m3fn_x4
ALU = mybir.AluOpType
ACT = mybir.ActivationFunctionType

P = 128
PACK = 4
LAST = PACK - 1
QUADRANT = 32
BLOCK_PARTITIONS = 8
TABLE = 2048
S = 512
HALF = S // 2
LIST_COLS = S // 16
LINE = 16
RUN = 4
SIXTEENTH = 0.0625
VECTOR_SHARE = 168
VECTOR_BANKS = 2
FLOPS = 2 * 2 * 512 * 512 * 512


def tile_picked_ringdiftrack_none_po_kernel(
    tc, x_words, x_scales, d_words, d_scales, gs, offs, k1, n1, n2, n3, out_0, out_1, out_2
):
    nc = tc.nc
    with ExitStack() as ctx:
        lists = ctx.enter_context(tc.tile_pool(name="lists", bufs=1))
        keep = ctx.enter_context(tc.tile_pool(name="keep", bufs=1))
        psum = ctx.enter_context(tc.psum_pool(name="psum", bufs=1))

        def list_tile(name):
            return lists.tile([P, LIST_COLS], U16, name=name)

        def half_of(list_t, half):
            return list_t[:, half * LIST_COLS // 2 : (half + 1) * LIST_COLS // 2]

        def cols(half):
            return slice(half * HALF, (half + 1) * HALF)

        def word_rows(words):
            return words[0].rearrange("p n t -> p (n t)").bitcast(I32)

        k1_t, offs_t, n1_t, n2_t, n3_t = (list_tile(n) for n in ("k1_t", "offs_t", "n1_t", "n2_t", "n3_t"))
        d_word_table = keep.tile([P, TABLE], U32, name="d_word_table")
        x_word_table = keep.tile([P, TABLE], U32, name="x_word_table")
        d_scale_table = keep.tile([P, TABLE], U8, name="d_scale_table")
        x_scale_table = keep.tile([P, TABLE], U8, name="x_scale_table")
        d_plane = keep.tile([P, S], U8, name="d_plane", align_bytes=64)
        gs_t = keep.tile([P, PACK], F32, name="gs_t")
        gain = keep.tile([P, PACK], F32, name="gain")

        nc.vector.memset(d_scale_table[:].bitcast(I32), 0)
        nc.vector.memset(x_scale_table[:].bitcast(I32), 0)
        warm = keep.tile([P, 2], F32, name="warm")
        nc.vector.memset(warm[:, 0:1], 0.0)

        nc.sync.dma_start(k1_t[:], k1)
        nc.sync.dma_start(d_scale_table[:].bitcast(I32)[0:P:BLOCK_PARTITIONS, :], d_scales[0].bitcast(I32))
        nc.sync.dma_start(offs_t[:], offs)
        nc.sync.dma_start(d_word_table[:].bitcast(I32), word_rows(d_words))
        nc.sync.dma_start(n1_t[:], n1)
        nc.sync.dma_start(gs_t[:], gs.rearrange("(p t) o -> p (t o)", t=PACK))
        nc.sync.dma_start(x_word_table[:].bitcast(I32), word_rows(x_words))
        nc.sync.dma_start(n2_t[:], n2)
        nc.sync.dma_start(n3_t[:], n3)
        for q in range(P // QUADRANT):
            nc.scalar.dma_start(
                x_scale_table[:].bitcast(I32)[QUADRANT * q : QUADRANT * q + PACK, :],
                x_scales[0, PACK * q : PACK * q + PACK, :].bitcast(I32),
            )
        nc.scalar.activation(warm[:, 1:2], warm[:, 0:1], ACT.Sigmoid)
        nc.scalar.activation(gain[:], gs_t[:], ACT.Copy, scale=-SIXTEENTH)

        def deal(dealt, picked, per_line):
            nc.vector.tensor_copy(
                dealt.rearrange("p (t c i) -> p c t i", t=PACK, i=per_line),
                picked.rearrange("p (c i t) -> p c t i", t=PACK, i=per_line),
            )

        d_scales_picked = keep.tile([P, S], U8, name="d_scales_picked")
        nc.vector.tensor_copy(d_scales_picked[:], d_scale_table[:].indirect(k1_t[:]))
        deal(d_plane[:], d_scales_picked[:], LINE)
        for a in range(1, PACK):
            nc.scalar.dma_start(
                d_plane[:].bitcast(I32)[a:P:QUADRANT, :],
                d_plane[:].bitcast(I32)[BLOCK_PARTITIONS * a : P : QUADRANT, :],
            )

        d_words_picked = keep.tile([P, S], U32, name="d_words_picked", tag="picked", align_bytes=64)
        d_codes = keep.tile([P, S], U32, name="d_codes", align_bytes=64)
        nc.vector.tensor_copy(d_words_picked[:], d_word_table[:].indirect(k1_t[:]))
        deal(d_codes[:].bitcast(I32), d_words_picked[:].bitcast(I32), LINE // PACK)

        def product(t, half, codes, plane):
            bank = psum.tile([P, S], F32, name=f"bank{t}{half}")
            dealt = slice(t * P, (t + 1) * P)
            nc.tensor.matmul_mx(
                out=bank[:, :HALF],
                lhsT=d_codes[:, dealt].bitcast(FP8X4),
                lhsT_scale=d_plane[:, dealt],
                rhs=codes.bitcast(FP8X4),
                rhs_scale=plane,
                start=True,
                stop=True,
            )
            return bank[:, :HALF]

        x_codes = [keep.tile([P, HALF], U32, name=f"x_codes{half}", align_bytes=64) for half in range(2)]
        x_plane = keep.tile([P, S], U8, name="x_plane", tag="picked", align_bytes=64)
        nc.vector.tensor_copy(x_plane[:], x_scale_table[:].indirect(offs_t[:]))
        for half in range(2):
            nc.vector.tensor_copy(x_codes[half][:], x_word_table[:].indirect(half_of(offs_t, half)))
        first = {}
        for pair in range(PACK // 2):
            for half in range(2):
                for t in (2 * pair, 2 * pair + 1):
                    first[t, half] = product(t, half, x_codes[half][:], x_plane[:, cols(half)])

        window = [keep.tile([P, S], F32, name=f"window{t}") for t in range(PACK)]
        z = [keep.tile([P, (PACK + half) * HALF], F32, name=f"z{half}", align_bytes=64) for half in range(2)]
        own = [
            [
                z[0][:, :HALF] if (t, half) == (LAST, 1) else keep.tile([P, HALF], F32, name=f"own{t}{half}")[:]
                for half in range(2)
            ]
            for t in range(PACK)
        ]

        def leave_first(out, t, half):
            nc.scalar.activation(out, first[t, half], ACT.Copy, scale=gain[:, t : t + 1])

        def difference(t, half):
            nc.vector.tensor_tensor(
                z[half][:, t * HALF : (t + 1) * HALF],
                window[t][:].indirect(half_of(n1_t, half)),
                own[t][half],
                ALU.subtract,
            )

        def z_tiles(half):
            return z[half][:, : PACK * HALF].rearrange("p (t c) -> p t c", t=PACK)

        def rounded_tile(name):
            return keep.tile([P, HALF * PACK], BF16, name=name, align_bytes=64)[:]

        def interleave(copy, rounded, tiles, part):
            copy(
                rounded.rearrange("p (c t) -> p c t", t=PACK)[:, part, :].rearrange("p (c i) t -> p c t i", i=RUN),
                tiles[:, :, part].rearrange("p t (c i) -> p c t i", i=RUN),
            )

        def interleave_on_scalar(rounded, tiles):
            interleave(nc.scalar.copy, rounded, tiles, slice(0, HALF))
            return rounded

        def interleave_on_both(rounded, tiles):
            interleave(nc.vector.tensor_copy, rounded, tiles, slice(0, VECTOR_SHARE))
            interleave(nc.scalar.copy, rounded, tiles, slice(VECTOR_SHARE, HALF))
            return rounded

        for t in range(PACK):
            leave_first(window[t][:, cols(0)], t, 0)
            leave_first(own[t][0], t, 0)
            if t < VECTOR_BANKS:
                nc.vector.tensor_scalar(window[t][:, cols(1)], first[t, 1], gain[:, t : t + 1], None, ALU.mult)
            else:
                leave_first(window[t][:, cols(1)], t, 1)
        for t in range(PACK):
            difference(t, 0)
        for t in range(LAST):
            leave_first(own[t][1], t, 1)
        z_codes = [keep.tile([P, HALF], U32, name=f"z_codes{half}", align_bytes=64) for half in range(2)]
        z_plane = [keep.tile([P, HALF], U8, name=f"z_plane{half}", align_bytes=64) for half in range(2)]
        h2 = [keep.tile([P, S], F32, name=f"h2{t}") for t in range(PACK)]

        def quantise_z(half, rounded):
            nc.vector.quantize_mx(z_codes[half][:].bitcast(FP8X4), z_plane[half][:], rounded)

        def second_product(half):
            return [product(t, half, z_codes[half][:], z_plane[half][:]) for t in range(PACK)]

        def leave_second(t, half, bank):
            nc.scalar.activation(h2[t][:, cols(half)], bank, ACT.Copy, scale=SIXTEENTH)

        z_rounded0 = interleave_on_scalar(z[1][:, LAST * HALF :].bitcast(BF16), z_tiles(0))
        leave_first(own[LAST][1], LAST, 1)
        for t in range(LAST):
            difference(t, 1)
        quantise_z(0, z_rounded0)
        difference(LAST, 1)

        second0 = second_product(0)
        z_rounded1 = interleave_on_both(rounded_tile("z_rounded1"), z_tiles(1))
        for t in range(PACK):
            leave_second(t, 0, second0[t])
        quantise_z(1, z_rounded1)
        second1 = second_product(1)
        leave_second(0, 1, second1[0])
        nc.vector.tensor_scalar(h2[1][:, cols(1)], second1[1], SIXTEENTH, None, ALU.mult)

        result = [keep.tile([P, PACK, HALF], F32, name=f"result{half}") for half in range(2)]
        out_codes = keep.tile([P, S], U32, name="out_codes", align_bytes=64)
        out_plane = keep.tile([P, S], U8, name="out_plane", align_bytes=64)
        out_rows = out_0.rearrange("(p t) c -> p t c", t=PACK)
        out_words = word_rows(out_1)
        first_gate = keep.tile([P, HALF], F32, name="first_gate")

        def blend_terms(t, half, gate):
            pulled = keep.tile([P, HALF], F32, name=f"pulled{t}{half}")
            kept = keep.tile([P, HALF], F32, name=f"kept{t}{half}")
            nc.scalar.activation(gate, h2[t][:].indirect(half_of(n2_t, half)), ACT.Sigmoid)
            if (t, half) == (0, 0):
                fetched = keep.tile([P, HALF], F32, name="fetched")
                nc.vector.tensor_copy(fetched[:], h2[t][:].indirect(half_of(n3_t, half)))
                nc.vector.tensor_tensor(pulled[:], fetched[:], gate, ALU.mult)
            else:
                nc.vector.tensor_tensor(pulled[:], h2[t][:].indirect(half_of(n3_t, half)), gate, ALU.mult)
            nc.vector.scalar_tensor_tensor(kept[:], gate, 1.0, h2[t][:, cols(half)], ALU.subtract, ALU.mult)
            return pulled, kept

        def blend_end(t, half, pulled, kept):
            nc.vector.tensor_tensor(result[half][:, t, :], pulled[:], kept[:], ALU.subtract)
            nc.sync.dma_start(out_rows[:, t, cols(half)], result[half][:, t, :])

        def quantise_out(half, rounded):
            nc.vector.quantize_mx(out_codes[:, cols(half)].bitcast(FP8X4), out_plane[:, cols(half)], rounded)
            nc.sync.dma_start(out_words[:, cols(half)], out_codes[:, cols(half)].bitcast(I32))

        gate = first_gate[:]
        unfinished = []
        for half in range(2):
            for t in range(PACK):
                if half == 0 and t >= 2:
                    leave_second(t, 1, second1[t])
                terms = blend_terms(t, half, gate)
                if unfinished:
                    blend_end(*unfinished.pop())
                unfinished.append((t, half) + terms)
                gate = result[half][:, t, :]
                if (t, half) == (0, 1):
                    out_rounded0 = interleave_on_scalar(rounded_tile("out_rounded0"), result[0][:])
                if (t, half) == (2, 1):
                    quantise_out(0, out_rounded0)
        blend_end(*unfinished.pop())
        quantise_out(1, interleave_on_both(rounded_tile("out_rounded1"), result[1][:]))
        for q in range(P // QUADRANT):
            (nc.scalar if q % 2 else nc.sync).dma_start(
                out_2[0, PACK * q : PACK * q + PACK, :].bitcast(I32),
                out_plane[:].bitcast(I32)[QUADRANT * q : QUADRANT * q + PACK, :],
            )
